import numpy as np
import ml_dtypes


def mxq(x, axis, fmt="e4m3"):
    dtype, down = {"e4m3": (ml_dtypes.float8_e4m3fn, 7), "e5m2": (ml_dtypes.float8_e5m2, 14)}[fmt]
    v = np.moveaxis(np.asarray(x, np.float32).astype(ml_dtypes.bfloat16).astype(np.float64), axis, -1)
    blocks = v.reshape(v.shape[:-1] + (-1, 32))
    amax = np.abs(blocks).max(-1, keepdims=True)
    byte = np.maximum(np.where(amax > 0, np.frexp(amax)[1] - 1 + 127, 0) - down, 1)
    scale = np.exp2(byte - 127.0)
    codes = (blocks / scale).astype(np.float32).astype(dtype).astype(np.float64)
    return np.moveaxis((codes * scale).reshape(v.shape), -1, axis)


WIDE = False


def mx_kscale(k):
    if not WIDE:
        return np.ones(k)
    levels = np.array([30, -30])
    if k % 512:
        return np.exp2(np.random.permutation(np.resize(levels, k // 32))).repeat(32)
    a = np.empty((k // 512, 16))
    for p in range(k // 512):
        a[p, :8] = np.random.permutation(np.resize(levels, 8))
        for g in range(8):
            far = levels[np.abs(levels - a[p, g]) >= 10]
            a[p, g + 8] = far[np.random.randint(len(far))]
    return np.exp2(a.ravel()).repeat(32)


def f64(x):
    return np.asarray(x).astype(np.float64)


def striped(idx):
    return np.tile(np.asarray(idx).reshape(-1, 16).T, (8, 1)).astype(np.uint16)


def unstriped(offs):
    return offs[:16].T.reshape(-1).astype(np.int64)


E2M1 = np.array([0.0, 0.5, 1.0, 1.5, 2.0, 3.0, 4.0, 6.0, -0.0, -0.5, -1.0, -1.5, -2.0, -3.0, -4.0, -6.0])


def pack_weight(w, fmt):
    k, n = w.shape
    w = f64(np.asarray(w, np.float32).astype(ml_dtypes.bfloat16)).reshape(k // 32, 32, n)
    amax = np.abs(w).max(1)
    if fmt in ("e4m3", "e5m2"):
        byte = np.frexp(amax)[1] - 1 + 127 - (7 if fmt == "e4m3" else 14)
    else:
        mant, ex = np.frexp(amax / 6.0)
        byte = np.where(mant > 0.5, ex, ex - 1) + 127
    byte = np.clip(np.where(amax > 0, byte, 1), 1, 254)
    scaled = (w * np.exp2(127.0 - byte)[:, None, :]).reshape(k, n).astype(np.float32)
    by_word = np.ascontiguousarray(scaled.reshape(k // 512, 128, 4, n).transpose(0, 1, 3, 2))
    if fmt in ("e4m3", "e5m2"):
        words = by_word.astype(ml_dtypes.float8_e4m3fn if fmt == "e4m3" else ml_dtypes.float8_e5m2).view(np.uint8)
    else:
        c = by_word.astype(ml_dtypes.float4_e2m1fn).view(np.uint8) & 0xF
        words = (c[..., 0::2] | (c[..., 1::2] << 4)).reshape(k // 512, 128, 2 * n)
    return np.ascontiguousarray(words), np.ascontiguousarray(byte.astype(np.uint8).reshape(k // 512, 16, n))


def unpack_weight(words, scales, fmt):
    g, _, n = scales.shape
    words = np.ascontiguousarray(words).reshape(g, 128, n, -1)
    if fmt in ("e4m3", "e5m2"):
        vals = words.view(ml_dtypes.float8_e4m3fn if fmt == "e4m3" else ml_dtypes.float8_e5m2).astype(np.float64)
    else:
        nib = np.empty((g, 128, n, 4), np.uint8)
        nib[..., 0::2] = words & 0xF
        nib[..., 1::2] = words >> 4
        vals = E2M1[nib]
    vals = vals * np.repeat(np.exp2(scales.astype(np.float64) - 127.0), 8, axis=1)[..., None]
    return vals.transpose(0, 1, 3, 2).reshape(g * 512, n)


K, F, T, Z, J, R, C, N, L = 512, 512, 1024, 1024, 256, 512, 512, 256, 512


def setup_inputs():
    n = np.random.standard_normal
    idx = np.random.permutation(T)[:J]
    idx2 = np.random.permutation(Z)[:J]
    idx3 = np.random.permutation(C)[:J]
    idx4 = np.random.permutation(C)[:J]
    fk = mx_kscale(K)
    fr = mx_kscale(R)
    ff = mx_kscale(F)
    fl = mx_kscale(L)
    xtp = pack_weight(n((K, T)) / fk[:, None], "e4m3")
    wp = pack_weight(n((K, R)) * 1 / np.sqrt(K) * fk[:, None] * fr, "e2m1")
    xop = pack_weight(n((F, Z)) / ff[:, None], "e2m1")
    w2p = pack_weight(n((F, R)) * 1 / np.sqrt(F) * ff[:, None] * fr, "e5m2")
    wbp = pack_weight(n((R, N)) * 1 / np.sqrt(R) / fr[:, None], "e5m2")
    sxp = pack_weight(n((L, J)) / fl[:, None], "e2m1")
    wsp = pack_weight(n((L, N)) * 1 / np.sqrt(L) * fl[:, None], "e5m2")
    return {
        "xt_words": xtp[0],
        "xt_scales": xtp[1],
        "w_words": wp[0],
        "w_scales": wp[1],
        "xo_words": xop[0],
        "xo_scales": xop[1],
        "w2_words": w2p[0],
        "w2_scales": w2p[1],
        "wb_words": wbp[0],
        "wb_scales": wbp[1],
        "sx_words": sxp[0],
        "sx_scales": sxp[1],
        "ws_words": wsp[0],
        "ws_scales": wsp[1],
        "offs": striped(idx),
        "offs2": striped(idx2),
        "offs3": striped(idx3),
        "offs4": striped(idx4),
    }


def reference(xt_words, xt_scales, w_words, w_scales, xo_words, xo_scales, w2_words, w2_scales, wb_words, wb_scales, sx_words, sx_scales, ws_words, ws_scales, offs, offs2, offs3, offs4):
    idx = unstriped(offs)
    idx2 = unstriped(offs2)
    idx3 = unstriped(offs3)
    idx4 = unstriped(offs4)
    xtu = unpack_weight(xt_words, xt_scales, "e4m3")
    wu = unpack_weight(w_words, w_scales, "e2m1")
    xou = unpack_weight(xo_words, xo_scales, "e2m1")
    w2u = unpack_weight(w2_words, w2_scales, "e5m2")
    wbu = unpack_weight(wb_words, wb_scales, "e5m2")
    sxu = unpack_weight(sx_words, sx_scales, "e2m1")
    wsu = unpack_weight(ws_words, ws_scales, "e5m2")
    xtidxg = xtu[:, idx]
    a = wu.T @ xtidxg
    xoidx2g = xou[:, idx2]
    b = w2u.T @ xoidx2g
    pw = np.zeros((R, C))
    pw[:, idx3] = a
    hid = np.maximum(pw[:, idx4], b)
    hidq = mxq(hid, 0, "e4m3")
    y = wbu.T @ hidq + wsu.T @ sxu
    return y

@@ -1,0 +1,181 @@
+from contextlib import ExitStack
+
+import concourse.mybir as mybir
+
+F32 = mybir.dt.float32
+BF16 = mybir.dt.bfloat16
+I32 = mybir.dt.int32
+U32 = mybir.dt.uint32
+U16 = mybir.dt.uint16
+U8 = mybir.dt.uint8
+E4M3 = mybir.dt.float8_e4m3fn_x4
+E5M2 = mybir.dt.float8_e5m2_x4
+E2M1 = mybir.dt.float4_e2m1fn_x4
+COPY = mybir.ActivationFunctionType.Copy
+MAX = mybir.AluOpType.max
+
+P = 128
+PACK = 4
+TOKENS, NOTES, SLOTS, HIDDEN, BOARD, OUTS = 1024, 1024, 256, 512, 512, 256
+HALF = SLOTS // 2
+FLOPS = 2 * 512 * SLOTS * (2 * HIDDEN + 2 * OUTS)
+
+
+def tile_list_twotab_board_skip_plain_kernel(
+    tc, xt_words, xt_scales, w_words, w_scales, xo_words, xo_scales, w2_words, w2_scales,
+    wb_words, wb_scales, sx_words, sx_scales, ws_words, ws_scales, offs, offs2, offs3, offs4, out,
+):
+    nc = tc.nc
+    with ExitStack() as ctx:
+        lists = ctx.enter_context(tc.tile_pool(name="lists", bufs=1))
+        keep = ctx.enter_context(tc.tile_pool(name="keep", bufs=1))
+        psum = ctx.enter_context(tc.psum_pool(name="psum", bufs=1))
+
+        def load_list(name, source):
+            tile = lists.tile([P, SLOTS // 16], U16, name=name)
+            nc.sync.dma_start(tile[:], source)
+            return tile
+
+        def load_words(name, source, columns, dtype, queue=nc.sync):
+            tile = keep.tile([P, columns], dtype, name=name, align_bytes=64)
+            rows = source[0]
+            if rows.ndim == 3:
+                rows = rows.rearrange("p c t -> p (c t)")
+            queue.dma_start(tile[:].bitcast(I32), rows.bitcast(I32))
+            return tile
+
+        def zeroed_plane(name, columns):
+            tile = keep.tile([P, columns], U8, name=name, align_bytes=64)
+            nc.vector.memset(tile[:].bitcast(I32), 0)
+            return tile
+
+        def load_scales(tile, source):
+            for r in range(4):
+                nc.sync.dma_start(tile[r:P:32, :].bitcast(I32), source[0, r:16:4, :].bitcast(I32))
+
+        w_s = zeroed_plane("w_s", HIDDEN)
+        xt_s = zeroed_plane("xt_s", TOKENS)
+        xo_s = zeroed_plane("xo_s", NOTES)
+        w2_s = zeroed_plane("w2_s", HIDDEN)
+        ws_s = zeroed_plane("ws_s", OUTS)
+        sx_s = zeroed_plane("sx_s", SLOTS)
+        wb_s = zeroed_plane("wb_s", OUTS)
+
+        xt_w = load_words("xt_w", xt_words, TOKENS, U32, nc.scalar)
+        w_w = load_words("w_w", w_words, HIDDEN, U16, nc.scalar)
+        idx = load_list("idx", offs)
+        load_scales(w_s, w_scales)
+        load_scales(xt_s, xt_scales)
+        idx3 = load_list("idx3", offs3)
+        idx2 = load_list("idx2", offs2)
+        xo_w = load_words("xo_w", xo_words, NOTES, U16)
+        load_scales(xo_s, xo_scales)
+        w2_w = load_words("w2_w", w2_words, HIDDEN, U32)
+        load_scales(w2_s, w2_scales)
+        idx4 = load_list("idx4", offs4)
+        ws_w = load_words("ws_w", ws_words, OUTS, U32)
+        load_scales(ws_s, ws_scales)
+        sx_w = load_words("sx_w", sx_words, SLOTS, U16)
+        load_scales(sx_s, sx_scales)
+        wb_w = load_words("wb_w", wb_words, OUTS, U32)
+        load_scales(wb_s, wb_scales)
+
+        pages = [keep.tile([P, BOARD], F32, name="page%d" % t) for t in range(PACK)]
+        for page in pages:
+            nc.vector.memset(page[:], 0.0)
+
+        def dealt(name, tile, dtype):
+            return keep.tile([P, HIDDEN], dtype, name=name, align_bytes=64)
+
+        def deal(copy, dst, src, run):
+            copy(
+                dst[:].rearrange("p (t c i) -> p c t i", t=PACK, i=run),
+                src[:].rearrange("p (c i t) -> p c t i", t=PACK, i=run),
+            )
+
+        def gathered(name, table, offsets, dtype):
+            tile = keep.tile([P, SLOTS], dtype, name=name, align_bytes=64)
+            nc.vector.tensor_copy(tile[:], table[:].indirect(offsets[:]))
+            return tile
+
+        w_wd = dealt("w_wd", w_w, U16)
+        w_sd = dealt("w_sd", w_s, U8)
+        deal(nc.scalar.copy, w_wd, w_w, 8)
+        deal(nc.vector.tensor_copy, w_sd, w_s, 16)
+        xt_wg = gathered("xt_wg", xt_w, idx, U32)
+        xt_sg = gathered("xt_sg", xt_s, idx, U8)
+
+        a_banks = [psum.tile([P, SLOTS], F32, name="a_bank%d" % t) for t in range(PACK)]
+        for t in range(PACK):
+            cols = slice(P * t, P * (t + 1))
+            nc.tensor.matmul_mx(
+                a_banks[t][:], lhsT=w_wd[:, cols].bitcast(E2M1), lhsT_scale=w_sd[:, cols],
+                rhs=xt_wg[:].bitcast(E4M3), rhs_scale=xt_sg[:], start=True, stop=True,
+            )
+
+        w2_wd = dealt("w2_wd", w2_w, U32)
+        w2_sd = dealt("w2_sd", w2_s, U8)
+        deal(nc.scalar.copy, w2_wd, w2_w, 4)
+        xo_wg = gathered("xo_wg", xo_w, idx2, U16)
+        xo_sg = gathered("xo_sg", xo_s, idx2, U8)
+        deal(nc.vector.tensor_copy, w2_sd, w2_s, 16)
+
+        a_sb = [keep.tile([P, SLOTS], F32, name="a_sb%d" % t) for t in range(PACK)]
+        for t in range(PACK):
+            nc.scalar.copy(a_sb[t][:], a_banks[t][:])
+
+        b_banks = [psum.tile([P, PACK, HALF], F32, name="b_bank%d" % h) for h in range(2)]
+        for h in range(2):
+            slots = slice(HALF * h, HALF * (h + 1))
+            for t in range(PACK):
+                cols = slice(P * t, P * (t + 1))
+                nc.tensor.matmul_mx(
+                    b_banks[h][:, t, :], lhsT=w2_wd[:, cols].bitcast(E5M2), lhsT_scale=w2_sd[:, cols],
+                    rhs=xo_wg[:, slots].bitcast(E2M1), rhs_scale=xo_sg[:, slots], start=True, stop=True,
+                )
+
+        y_banks = [psum.tile([P, SLOTS], F32, name="y_bank%d" % u) for u in range(2)]
+        for u in range(2):
+            cols = slice(P * u, P * (u + 1))
+            nc.tensor.matmul_mx(
+                y_banks[u][:], lhsT=ws_w[:, cols].bitcast(E5M2), lhsT_scale=ws_s[:, cols],
+                rhs=sx_w[:].bitcast(E2M1), rhs_scale=sx_s[:], start=True, stop=False,
+            )
+
+        picked = keep.tile([P, PACK, SLOTS], F32, name="picked")
+        for t in range(PACK):
+            if t % 2 == 0:
+                nc.vector.tensor_copy(pages[t][:].indirect(idx3[:]), a_sb[t][:])
+            else:
+                nc.scalar.activation(pages[t][:].indirect(idx3[:]), a_sb[t][:], COPY)
+        for t in range(PACK):
+            if t % 2 == 0:
+                nc.vector.tensor_copy(picked[:, t, :], pages[t][:].indirect(idx4[:]))
+            else:
+                nc.scalar.activation(picked[:, t, :], pages[t][:].indirect(idx4[:]), COPY)
+
+        hid = [keep.tile([P, HALF, PACK], BF16, name="hid%d" % h, align_bytes=64) for h in range(2)]
+        hid_w = [keep.tile([P, HALF], U32, name="hid_w%d" % h, align_bytes=64) for h in range(2)]
+        hid_s = [keep.tile([P, HALF], U8, name="hid_s%d" % h, align_bytes=64) for h in range(2)]
+        for h in range(2):
+            slots = slice(HALF * h, HALF * (h + 1))
+            nc.vector.tensor_tensor(
+                hid[h][:], picked[:, :, slots].rearrange("p t j -> p j t"),
+                b_banks[h][:].rearrange("p t j -> p j t"), MAX,
+            )
+        for h in range(2):
+            nc.vector.quantize_mx(hid_w[h][:].bitcast(E4M3), hid_s[h][:], hid[h][:].rearrange("p j t -> p (j t)"))
+        for h in range(2):
+            slots = slice(HALF * h, HALF * (h + 1))
+            for u in range(2):
+                cols = slice(P * u, P * (u + 1))
+                nc.tensor.matmul_mx(
+                    y_banks[u][:, slots], lhsT=wb_w[:, cols].bitcast(E5M2), lhsT_scale=wb_s[:, cols],
+                    rhs=hid_w[h][:].bitcast(E4M3), rhs_scale=hid_s[h][:], start=False, stop=(h == 1),
+                )
+
+        y_sb = [keep.tile([P, SLOTS], F32, name="y_sb%d" % u) for u in range(2)]
+        nc.vector.tensor_copy(y_sb[0][:], y_banks[0][:])
+        nc.sync.dma_start(out[0:P, :], y_sb[0][:])
+        nc.scalar.copy(y_sb[1][:], y_banks[1][:])
+        nc.scalar.dma_start(out[P : 2 * P, :], y_sb[1][:])

@@ -49,28 +49,34 @@ def tile_list_twotab_board_skip_plain_kernel(
             nc.vector.memset(tile[:].bitcast(I32), 0)
             return tile
 
-        def load_scales(tile, source):
+        def load_scales(tile, source, queue=nc.sync):
             for r in range(4):
-                nc.sync.dma_start(tile[r:P:32, :].bitcast(I32), source[0, r:16:4, :].bitcast(I32))
+                queue.dma_start(tile[r:P:32, :].bitcast(I32), source[0, r:16:4, :].bitcast(I32))
 
-        w_s = zeroed_plane("w_s", HIDDEN)
-        xt_s = zeroed_plane("xt_s", TOKENS)
+        def load_quadrant(tile, source, q):
+            columns = source.shape[2]
+            rows = source[0, 4 * q : 4 * q + 4, :].bitcast(I32).unsqueeze(0).to_broadcast([8, 4, columns // 4])
+            nc.sync.dma_start(tile[32 * q : 32 * q + 32, :].bitcast(I32), rows)
+
+        xt_s = keep.tile([P, TOKENS], U8, name="xt_s", align_bytes=64)
         xo_s = zeroed_plane("xo_s", NOTES)
+        w_s = zeroed_plane("w_s", HIDDEN)
         w2_s = zeroed_plane("w2_s", HIDDEN)
         ws_s = zeroed_plane("ws_s", OUTS)
         sx_s = zeroed_plane("sx_s", SLOTS)
         wb_s = zeroed_plane("wb_s", OUTS)
 
-        xt_w = load_words("xt_w", xt_words, TOKENS, U32, nc.scalar)
-        w_w = load_words("w_w", w_words, HIDDEN, U16, nc.scalar)
         idx = load_list("idx", offs)
+        for q in range(4):
+            load_quadrant(xt_s, xt_scales, q)
+        xt_w = load_words("xt_w", xt_words, TOKENS, U32)
+        w_w = load_words("w_w", w_words, HIDDEN, U16)
         load_scales(w_s, w_scales)
-        load_scales(xt_s, xt_scales)
-        idx3 = load_list("idx3", offs3)
-        idx2 = load_list("idx2", offs2)
-        xo_w = load_words("xo_w", xo_words, NOTES, U16)
-        load_scales(xo_s, xo_scales)
         w2_w = load_words("w2_w", w2_words, HIDDEN, U32)
+        idx2 = load_list("idx2", offs2)
+        idx3 = load_list("idx3", offs3)
+        xo_w = load_words("xo_w", xo_words, NOTES, U16)
+        load_scales(xo_s, xo_scales, nc.sync)
         load_scales(w2_s, w2_scales)
         idx4 = load_list("idx4", offs4)
         ws_w = load_words("ws_w", ws_words, OUTS, U32)
@@ -84,26 +90,29 @@ def tile_list_twotab_board_skip_plain_kernel(
         for page in pages:
             nc.vector.memset(page[:], 0.0)
 
-        def dealt(name, tile, dtype):
-            return keep.tile([P, HIDDEN], dtype, name=name, align_bytes=64)
-
-        def deal(copy, dst, src, run):
+        def deal(copy, name, src, dtype, run):
+            dst = keep.tile([P, HIDDEN], dtype, name=name, align_bytes=64)
             copy(
                 dst[:].rearrange("p (t c i) -> p c t i", t=PACK, i=run),
                 src[:].rearrange("p (c i t) -> p c t i", t=PACK, i=run),
             )
+            return dst
 
         def gathered(name, table, offsets, dtype):
             tile = keep.tile([P, SLOTS], dtype, name=name, align_bytes=64)
             nc.vector.tensor_copy(tile[:], table[:].indirect(offsets[:]))
             return tile
 
-        w_wd = dealt("w_wd", w_w, U16)
-        w_sd = dealt("w_sd", w_s, U8)
-        deal(nc.scalar.copy, w_wd, w_w, 8)
-        deal(nc.vector.tensor_copy, w_sd, w_s, 16)
-        xt_wg = gathered("xt_wg", xt_w, idx, U32)
+        def scalar_move(dst, src):
+            nc.scalar.activation(dst, src, COPY)
+
+        w_wd = deal(nc.scalar.copy, "w_wd", w_w, U16, 8)
         xt_sg = gathered("xt_sg", xt_s, idx, U8)
+        xt_wg = gathered("xt_wg", xt_w, idx, U32)
+        w_sd = keep.tile([P, HIDDEN], U8, name="w_sd", align_bytes=64)
+        w_s_by_t = w_s[:].rearrange("p (m t) -> p t m", t=PACK)
+        nc.vector.tensor_copy(w_sd[:, 0:P], w_s_by_t[:, 0, :])
+        nc.vector.tensor_copy(w_sd[:, P:HIDDEN].rearrange("p (t m) -> p t m", t=PACK - 1), w_s_by_t[:, 1:PACK, :])
 
         a_banks = [psum.tile([P, SLOTS], F32, name="a_bank%d" % t) for t in range(PACK)]
         for t in range(PACK):
@@ -113,16 +122,20 @@ def tile_list_twotab_board_skip_plain_kernel(
                 rhs=xt_wg[:].bitcast(E4M3), rhs_scale=xt_sg[:], start=True, stop=True,
             )
 
-        w2_wd = dealt("w2_wd", w2_w, U32)
-        w2_sd = dealt("w2_sd", w2_s, U8)
-        deal(nc.scalar.copy, w2_wd, w2_w, 4)
+        a_sb = [keep.tile([P, SLOTS], F32, name="a_sb%d" % t) for t in range(PACK)]
+        nc.vector.tensor_copy(a_sb[0][:], a_banks[0][:])
+        for t in range(1, PACK):
+            nc.scalar.copy(a_sb[t][:], a_banks[t][:])
+        nc.vector.tensor_copy(pages[0][:].indirect(idx3[:]), a_sb[0][:])
+        scalar_move(pages[1][:].indirect(idx3[:]), a_sb[1][:])
+        nc.vector.tensor_copy(pages[2][:].indirect(idx3[:, 0:8]), a_sb[2][:, 0:HALF])
+        scalar_move(pages[3][:].indirect(idx3[:]), a_sb[3][:])
+        scalar_move(pages[2][:].indirect(idx3[:, 8:16]), a_sb[2][:, HALF:SLOTS])
+
         xo_wg = gathered("xo_wg", xo_w, idx2, U16)
         xo_sg = gathered("xo_sg", xo_s, idx2, U8)
-        deal(nc.vector.tensor_copy, w2_sd, w2_s, 16)
-
-        a_sb = [keep.tile([P, SLOTS], F32, name="a_sb%d" % t) for t in range(PACK)]
-        for t in range(PACK):
-            nc.scalar.copy(a_sb[t][:], a_banks[t][:])
+        w2_wd = deal(nc.scalar.copy, "w2_wd", w2_w, U32, 4)
+        w2_sd = deal(nc.vector.tensor_copy, "w2_sd", w2_s, U8, 16)
 
         b_banks = [psum.tile([P, PACK, HALF], F32, name="b_bank%d" % h) for h in range(2)]
         for h in range(2):
@@ -134,25 +147,22 @@ def tile_list_twotab_board_skip_plain_kernel(
                     rhs=xo_wg[:, slots].bitcast(E2M1), rhs_scale=xo_sg[:, slots], start=True, stop=True,
                 )
 
-        y_banks = [psum.tile([P, SLOTS], F32, name="y_bank%d" % u) for u in range(2)]
-        for u in range(2):
-            cols = slice(P * u, P * (u + 1))
-            nc.tensor.matmul_mx(
-                y_banks[u][:], lhsT=ws_w[:, cols].bitcast(E5M2), lhsT_scale=ws_s[:, cols],
-                rhs=sx_w[:].bitcast(E2M1), rhs_scale=sx_s[:], start=True, stop=False,
-            )
+        y_tags = ["y_bank0", "y_bank1", "a_bank0", "a_bank1"]
+        y_banks = {}
+        for h in range(2):
+            slots = slice(HALF * h, HALF * (h + 1))
+            for n in range(2):
+                cols = slice(P * n, P * (n + 1))
+                y_banks[h, n] = psum.tile([P, HALF], F32, name="y_bank%d%d" % (h, n), tag=y_tags[2 * h + n])
+                nc.tensor.matmul_mx(
+                    y_banks[h, n][:], lhsT=ws_w[:, cols].bitcast(E5M2), lhsT_scale=ws_s[:, cols],
+                    rhs=sx_w[:, slots].bitcast(E2M1), rhs_scale=sx_s[:, slots], start=True, stop=False,
+                )
 
         picked = keep.tile([P, PACK, SLOTS], F32, name="picked")
-        for t in range(PACK):
-            if t % 2 == 0:
-                nc.vector.tensor_copy(pages[t][:].indirect(idx3[:]), a_sb[t][:])
-            else:
-                nc.scalar.activation(pages[t][:].indirect(idx3[:]), a_sb[t][:], COPY)
-        for t in range(PACK):
-            if t % 2 == 0:
-                nc.vector.tensor_copy(picked[:, t, :], pages[t][:].indirect(idx4[:]))
-            else:
-                nc.scalar.activation(picked[:, t, :], pages[t][:].indirect(idx4[:]), COPY)
+        for t in (0, 1, 3, 2):
+            pick = scalar_move if t == 1 else nc.vector.tensor_copy
+            pick(picked[:, t, :], pages[t][:].indirect(idx4[:]))
 
         hid = [keep.tile([P, HALF, PACK], BF16, name="hid%d" % h, align_bytes=64) for h in range(2)]
         hid_w = [keep.tile([P, HALF], U32, name="hid_w%d" % h, align_bytes=64) for h in range(2)]
@@ -165,17 +175,16 @@ def tile_list_twotab_board_skip_plain_kernel(
             )
         for h in range(2):
             nc.vector.quantize_mx(hid_w[h][:].bitcast(E4M3), hid_s[h][:], hid[h][:].rearrange("p j t -> p (j t)"))
+        y_sb = [keep.tile([P, SLOTS], F32, name="y_sb%d" % n) for n in range(2)]
         for h in range(2):
             slots = slice(HALF * h, HALF * (h + 1))
-            for u in range(2):
-                cols = slice(P * u, P * (u + 1))
+            for n in range(2):
+                cols = slice(P * n, P * (n + 1))
                 nc.tensor.matmul_mx(
-                    y_banks[u][:, slots], lhsT=wb_w[:, cols].bitcast(E5M2), lhsT_scale=wb_s[:, cols],
-                    rhs=hid_w[h][:].bitcast(E4M3), rhs_scale=hid_s[h][:], start=False, stop=(h == 1),
+                    y_banks[h, n][:], lhsT=wb_w[:, cols].bitcast(E5M2), lhsT_scale=wb_s[:, cols],
+                    rhs=hid_w[h][:].bitcast(E4M3), rhs_scale=hid_s[h][:], start=False, stop=True,
                 )
-
-        y_sb = [keep.tile([P, SLOTS], F32, name="y_sb%d" % u) for u in range(2)]
-        nc.vector.tensor_copy(y_sb[0][:], y_banks[0][:])
+            nc.vector.tensor_copy(y_sb[0][:, slots], y_banks[h, 0][:])
+            nc.scalar.copy(y_sb[1][:, slots], y_banks[h, 1][:])
         nc.sync.dma_start(out[0:P, :], y_sb[0][:])
-        nc.scalar.copy(y_sb[1][:], y_banks[1][:])
         nc.scalar.dma_start(out[P : 2 * P, :], y_sb[1][:])

@@ -53,10 +53,10 @@ def tile_list_twotab_board_skip_plain_kernel(
             for r in range(4):
                 queue.dma_start(tile[r:P:32, :].bitcast(I32), source[0, r:16:4, :].bitcast(I32))
 
-        def load_quadrant(tile, source, q):
+        def load_quadrant(tile, source, q, queue):
             columns = source.shape[2]
             rows = source[0, 4 * q : 4 * q + 4, :].bitcast(I32).unsqueeze(0).to_broadcast([8, 4, columns // 4])
-            nc.sync.dma_start(tile[32 * q : 32 * q + 32, :].bitcast(I32), rows)
+            queue.dma_start(tile[32 * q : 32 * q + 32, :].bitcast(I32), rows)
 
         xt_s = keep.tile([P, TOKENS], U8, name="xt_s", align_bytes=64)
         xo_s = zeroed_plane("xo_s", NOTES)
@@ -68,7 +68,7 @@ def tile_list_twotab_board_skip_plain_kernel(
 
         idx = load_list("idx", offs)
         for q in range(4):
-            load_quadrant(xt_s, xt_scales, q)
+            load_quadrant(xt_s, xt_scales, q, nc.scalar if q < 2 else nc.sync)
         xt_w = load_words("xt_w", xt_words, TOKENS, U32)
         w_w = load_words("w_w", w_words, HIDDEN, U16)
         load_scales(w_s, w_scales)
@@ -159,10 +159,12 @@ def tile_list_twotab_board_skip_plain_kernel(
                     rhs=sx_w[:, slots].bitcast(E2M1), rhs_scale=sx_s[:, slots], start=True, stop=False,
                 )
 
-        picked = keep.tile([P, PACK, SLOTS], F32, name="picked")
-        for t in (0, 1, 3, 2):
-            pick = scalar_move if t == 1 else nc.vector.tensor_copy
-            pick(picked[:, t, :], pages[t][:].indirect(idx4[:]))
+        picked = [keep.tile([P, PACK, HALF], F32, name="picked%d" % h) for h in range(2)]
+        for h, t, pick in (
+            (0, 0, nc.vector.tensor_copy), (0, 3, nc.vector.tensor_copy), (0, 1, scalar_move), (1, 0, nc.vector.tensor_copy),
+            (0, 2, nc.vector.tensor_copy), (1, 1, scalar_move), (1, 3, scalar_move), (1, 2, scalar_move),
+        ):
+            pick(picked[h][:, t, :], pages[t][:].indirect(idx4[:, 8 * h : 8 * (h + 1)]))
 
         hid = [keep.tile([P, HALF, PACK], BF16, name="hid%d" % h, align_bytes=64) for h in range(2)]
         hid_w = [keep.tile([P, HALF], U32, name="hid_w%d" % h, align_bytes=64) for h in range(2)]
@@ -170,12 +172,12 @@ def tile_list_twotab_board_skip_plain_kernel(
         for h in range(2):
             slots = slice(HALF * h, HALF * (h + 1))
             nc.vector.tensor_tensor(
-                hid[h][:], picked[:, :, slots].rearrange("p t j -> p j t"),
-                b_banks[h][:].rearrange("p t j -> p j t"), MAX,
+                hid[h][:].rearrange("p (c i) t -> p c t i", i=2),
+                picked[h][:].rearrange("p t (c i) -> p c t i", i=2),
+                b_banks[h][:].rearrange("p t (c i) -> p c t i", i=2), MAX,
             )
         for h in range(2):
             nc.vector.quantize_mx(hid_w[h][:].bitcast(E4M3), hid_s[h][:], hid[h][:].rearrange("p j t -> p (j t)"))
-        y_sb = [keep.tile([P, SLOTS], F32, name="y_sb%d" % n) for n in range(2)]
         for h in range(2):
             slots = slice(HALF * h, HALF * (h + 1))
             for n in range(2):
@@ -184,7 +186,10 @@ def tile_list_twotab_board_skip_plain_kernel(
                     y_banks[h, n][:], lhsT=wb_w[:, cols].bitcast(E5M2), lhsT_scale=wb_s[:, cols],
                     rhs=hid_w[h][:].bitcast(E4M3), rhs_scale=hid_s[h][:], start=False, stop=True,
                 )
-            nc.vector.tensor_copy(y_sb[0][:, slots], y_banks[h, 0][:])
-            nc.scalar.copy(y_sb[1][:, slots], y_banks[h, 1][:])
-        nc.sync.dma_start(out[0:P, :], y_sb[0][:])
-        nc.scalar.dma_start(out[P : 2 * P, :], y_sb[1][:])
+            for n in range(2):
+                y_sb = keep.tile([P, HALF], F32, name="y_sb%d%d" % (h, n))
+                last = h == 1
+                copy = nc.vector.tensor_copy if (last and n == 0) else nc.scalar.copy
+                queue = nc.scalar if (last and n == 1) else nc.sync
+                copy(y_sb[:], y_banks[h, n][:])
+                queue.dma_start(out[P * n : P * (n + 1), slots], y_sb[:])

from contextlib import ExitStack

import concourse.mybir as mybir

F32 = mybir.dt.float32
BF16 = mybir.dt.bfloat16
I32 = mybir.dt.int32
U32 = mybir.dt.uint32
U16 = mybir.dt.uint16
U8 = mybir.dt.uint8
E4M3 = mybir.dt.float8_e4m3fn_x4
E5M2 = mybir.dt.float8_e5m2_x4
E2M1 = mybir.dt.float4_e2m1fn_x4
COPY = mybir.ActivationFunctionType.Copy
MAX = mybir.AluOpType.max

P = 128
PACK = 4
TOKENS, NOTES, SLOTS, HIDDEN, BOARD, OUTS = 1024, 1024, 256, 512, 512, 256
HALF = SLOTS // 2
FLOPS = 2 * 512 * SLOTS * (2 * HIDDEN + 2 * OUTS)


def tile_list_twotab_board_skip_plain_kernel(
    tc, xt_words, xt_scales, w_words, w_scales, xo_words, xo_scales, w2_words, w2_scales,
    wb_words, wb_scales, sx_words, sx_scales, ws_words, ws_scales, offs, offs2, offs3, offs4, out,
):
    nc = tc.nc
    with ExitStack() as ctx:
        lists = ctx.enter_context(tc.tile_pool(name="lists", bufs=1))
        keep = ctx.enter_context(tc.tile_pool(name="keep", bufs=1))
        psum = ctx.enter_context(tc.psum_pool(name="psum", bufs=1))

        def load_list(name, source):
            tile = lists.tile([P, SLOTS // 16], U16, name=name)
            nc.sync.dma_start(tile[:], source)
            return tile

        def load_words(name, source, columns, dtype, queue=nc.sync):
            tile = keep.tile([P, columns], dtype, name=name, align_bytes=64)
            rows = source[0]
            if rows.ndim == 3:
                rows = rows.rearrange("p c t -> p (c t)")
            queue.dma_start(tile[:].bitcast(I32), rows.bitcast(I32))
            return tile

        def zeroed_plane(name, columns):
            tile = keep.tile([P, columns], U8, name=name, align_bytes=64)
            nc.vector.memset(tile[:].bitcast(I32), 0)
            return tile

        def load_scales(tile, source, queue=nc.sync):
            for r in range(4):
                queue.dma_start(tile[r:P:32, :].bitcast(I32), source[0, r:16:4, :].bitcast(I32))

        def load_quadrant(tile, source, q, queue):
            columns = source.shape[2]
            rows = source[0, 4 * q : 4 * q + 4, :].bitcast(I32).unsqueeze(0).to_broadcast([8, 4, columns // 4])
            queue.dma_start(tile[32 * q : 32 * q + 32, :].bitcast(I32), rows)

        xt_s = keep.tile([P, TOKENS], U8, name="xt_s", align_bytes=64)
        xo_s = zeroed_plane("xo_s", NOTES)
        w_s = zeroed_plane("w_s", HIDDEN)
        w2_s = zeroed_plane("w2_s", HIDDEN)
        ws_s = zeroed_plane("ws_s", OUTS)
        sx_s = zeroed_plane("sx_s", SLOTS)
        wb_s = zeroed_plane("wb_s", OUTS)

        idx = load_list("idx", offs)
        for q in range(4):
            load_quadrant(xt_s, xt_scales, q, nc.scalar if q < 2 else nc.sync)
        xt_w = load_words("xt_w", xt_words, TOKENS, U32)
        w_w = load_words("w_w", w_words, HIDDEN, U16)
        load_scales(w_s, w_scales)
        w2_w = load_words("w2_w", w2_words, HIDDEN, U32)
        idx2 = load_list("idx2", offs2)
        idx3 = load_list("idx3", offs3)
        xo_w = load_words("xo_w", xo_words, NOTES, U16)
        load_scales(xo_s, xo_scales, nc.sync)
        load_scales(w2_s, w2_scales)
        idx4 = load_list("idx4", offs4)
        ws_w = load_words("ws_w", ws_words, OUTS, U32)
        load_scales(ws_s, ws_scales)
        sx_w = load_words("sx_w", sx_words, SLOTS, U16)
        load_scales(sx_s, sx_scales)
        wb_w = load_words("wb_w", wb_words, OUTS, U32)
        load_scales(wb_s, wb_scales)

        pages = [keep.tile([P, BOARD], F32, name="page%d" % t) for t in range(PACK)]
        for page in pages:
            nc.vector.memset(page[:], 0.0)

        def deal(copy, name, src, dtype, run):
            dst = keep.tile([P, HIDDEN], dtype, name=name, align_bytes=64)
            copy(
                dst[:].rearrange("p (t c i) -> p c t i", t=PACK, i=run),
                src[:].rearrange("p (c i t) -> p c t i", t=PACK, i=run),
            )
            return dst

        def gathered(name, table, offsets, dtype):
            tile = keep.tile([P, SLOTS], dtype, name=name, align_bytes=64)
            nc.vector.tensor_copy(tile[:], table[:].indirect(offsets[:]))
            return tile

        def scalar_move(dst, src):
            nc.scalar.activation(dst, src, COPY)

        w_wd = deal(nc.scalar.copy, "w_wd", w_w, U16, 8)
        xt_sg = gathered("xt_sg", xt_s, idx, U8)
        xt_wg = gathered("xt_wg", xt_w, idx, U32)
        w_sd = keep.tile([P, HIDDEN], U8, name="w_sd", align_bytes=64)
        w_s_by_t = w_s[:].rearrange("p (m t) -> p t m", t=PACK)
        nc.vector.tensor_copy(w_sd[:, 0:P], w_s_by_t[:, 0, :])
        nc.vector.tensor_copy(w_sd[:, P:HIDDEN].rearrange("p (t m) -> p t m", t=PACK - 1), w_s_by_t[:, 1:PACK, :])

        a_banks = [psum.tile([P, SLOTS], F32, name="a_bank%d" % t) for t in range(PACK)]
        for t in range(PACK):
            cols = slice(P * t, P * (t + 1))
            nc.tensor.matmul_mx(
                a_banks[t][:], lhsT=w_wd[:, cols].bitcast(E2M1), lhsT_scale=w_sd[:, cols],
                rhs=xt_wg[:].bitcast(E4M3), rhs_scale=xt_sg[:], start=True, stop=True,
            )

        a_sb = [keep.tile([P, SLOTS], F32, name="a_sb%d" % t) for t in range(PACK)]
        nc.vector.tensor_copy(a_sb[0][:], a_banks[0][:])
        for t in range(1, PACK):
            nc.scalar.copy(a_sb[t][:], a_banks[t][:])
        nc.vector.tensor_copy(pages[0][:].indirect(idx3[:]), a_sb[0][:])
        scalar_move(pages[1][:].indirect(idx3[:]), a_sb[1][:])
        nc.vector.tensor_copy(pages[2][:].indirect(idx3[:, 0:8]), a_sb[2][:, 0:HALF])
        scalar_move(pages[3][:].indirect(idx3[:]), a_sb[3][:])
        scalar_move(pages[2][:].indirect(idx3[:, 8:16]), a_sb[2][:, HALF:SLOTS])

        xo_wg = gathered("xo_wg", xo_w, idx2, U16)
        xo_sg = gathered("xo_sg", xo_s, idx2, U8)
        w2_wd = deal(nc.scalar.copy, "w2_wd", w2_w, U32, 4)
        w2_sd = deal(nc.vector.tensor_copy, "w2_sd", w2_s, U8, 16)

        b_banks = [psum.tile([P, PACK, HALF], F32, name="b_bank%d" % h) for h in range(2)]
        for h in range(2):
            slots = slice(HALF * h, HALF * (h + 1))
            for t in range(PACK):
                cols = slice(P * t, P * (t + 1))
                nc.tensor.matmul_mx(
                    b_banks[h][:, t, :], lhsT=w2_wd[:, cols].bitcast(E5M2), lhsT_scale=w2_sd[:, cols],
                    rhs=xo_wg[:, slots].bitcast(E2M1), rhs_scale=xo_sg[:, slots], start=True, stop=True,
                )

        y_tags = ["y_bank0", "y_bank1", "a_bank0", "a_bank1"]
        y_banks = {}
        for h in range(2):
            slots = slice(HALF * h, HALF * (h + 1))
            for n in range(2):
                cols = slice(P * n, P * (n + 1))
                y_banks[h, n] = psum.tile([P, HALF], F32, name="y_bank%d%d" % (h, n), tag=y_tags[2 * h + n])
                nc.tensor.matmul_mx(
                    y_banks[h, n][:], lhsT=ws_w[:, cols].bitcast(E5M2), lhsT_scale=ws_s[:, cols],
                    rhs=sx_w[:, slots].bitcast(E2M1), rhs_scale=sx_s[:, slots], start=True, stop=False,
                )

        picked = [keep.tile([P, PACK, HALF], F32, name="picked%d" % h) for h in range(2)]
        for h, t, pick in (
            (0, 0, nc.vector.tensor_copy), (0, 3, nc.vector.tensor_copy), (0, 1, scalar_move), (1, 0, nc.vector.tensor_copy),
            (0, 2, nc.vector.tensor_copy), (1, 1, scalar_move), (1, 3, scalar_move), (1, 2, scalar_move),
        ):
            pick(picked[h][:, t, :], pages[t][:].indirect(idx4[:, 8 * h : 8 * (h + 1)]))

        hid = [keep.tile([P, HALF, PACK], BF16, name="hid%d" % h, align_bytes=64) for h in range(2)]
        hid_w = [keep.tile([P, HALF], U32, name="hid_w%d" % h, align_bytes=64) for h in range(2)]
        hid_s = [keep.tile([P, HALF], U8, name="hid_s%d" % h, align_bytes=64) for h in range(2)]
        for h in range(2):
            slots = slice(HALF * h, HALF * (h + 1))
            nc.vector.tensor_tensor(
                hid[h][:].rearrange("p (c i) t -> p c t i", i=2),
                picked[h][:].rearrange("p t (c i) -> p c t i", i=2),
                b_banks[h][:].rearrange("p t (c i) -> p c t i", i=2), MAX,
            )
        for h in range(2):
            nc.vector.quantize_mx(hid_w[h][:].bitcast(E4M3), hid_s[h][:], hid[h][:].rearrange("p j t -> p (j t)"))
        for h in range(2):
            slots = slice(HALF * h, HALF * (h + 1))
            for n in range(2):
                cols = slice(P * n, P * (n + 1))
                nc.tensor.matmul_mx(
                    y_banks[h, n][:], lhsT=wb_w[:, cols].bitcast(E5M2), lhsT_scale=wb_s[:, cols],
                    rhs=hid_w[h][:].bitcast(E4M3), rhs_scale=hid_s[h][:], start=False, stop=True,
                )
            for n in range(2):
                y_sb = keep.tile([P, HALF], F32, name="y_sb%d%d" % (h, n))
                last = h == 1
                copy = nc.vector.tensor_copy if (last and n == 0) else nc.scalar.copy
                queue = nc.scalar if (last and n == 1) else nc.sync
                copy(y_sb[:], y_banks[h, n][:])
                queue.dma_start(out[P * n : P * (n + 1), slots], y_sb[:])
